import numpy as np
import ml_dtypes


def mxq(x, axis, fmt="e4m3"):
    dtype, down = {"e4m3": (ml_dtypes.float8_e4m3fn, 7), "e5m2": (ml_dtypes.float8_e5m2, 14)}[fmt]
    v = np.moveaxis(np.asarray(x, np.float32).astype(ml_dtypes.bfloat16).astype(np.float64), axis, -1)
    blocks = v.reshape(v.shape[:-1] + (-1, 32))
    amax = np.abs(blocks).max(-1, keepdims=True)
    byte = np.maximum(np.where(amax > 0, np.frexp(amax)[1] - 1 + 127, 0) - down, 1)
    scale = np.exp2(byte - 127.0)
    codes = (blocks / scale).astype(np.float32).astype(dtype).astype(np.float64)
    return np.moveaxis((codes * scale).reshape(v.shape), -1, axis)


WIDE = False


def mx_kscale(k):
    if not WIDE:
        return np.ones(k)
    levels = np.array([10, -10, 5, -5, 0])
    if k % 512:
        return np.exp2(np.random.permutation(np.resize(levels, k // 32))).repeat(32)
    a = np.empty((k // 512, 16))
    for p in range(k // 512):
        a[p, :8] = np.random.permutation(np.resize(levels, 8))
        for g in range(8):
            far = levels[np.abs(levels - a[p, g]) >= 10]
            a[p, g + 8] = far[np.random.randint(len(far))]
    return np.exp2(a.ravel()).repeat(32)


def f64(x):
    return np.asarray(x).astype(np.float64)


def striped(idx):
    return np.tile(idx.reshape(-1, 16).T, (8, 1)).astype(np.uint16)


def unstriped(offs):
    return offs[:16].T.reshape(-1).astype(np.int64)


E2M1 = np.array([0.0, 0.5, 1.0, 1.5, 2.0, 3.0, 4.0, 6.0, -0.0, -0.5, -1.0, -1.5, -2.0, -3.0, -4.0, -6.0])


def pack_weight(w, fmt):
    k, n = w.shape
    w = f64(np.asarray(w, np.float32).astype(ml_dtypes.bfloat16)).reshape(k // 32, 32, n)
    amax = np.abs(w).max(1)
    if fmt == "e4m3":
        byte = np.frexp(amax)[1] - 1 + 127 - 7
    else:
        mant, ex = np.frexp(amax / 6.0)
        byte = np.where(mant > 0.5, ex, ex - 1) + 127
    byte = np.clip(np.where(amax > 0, byte, 1), 1, 254)
    scaled = (w * np.exp2(127.0 - byte)[:, None, :]).reshape(k, n).astype(np.float32)
    by_word = np.ascontiguousarray(scaled.reshape(k // 512, 128, 4, n).transpose(0, 1, 3, 2))
    if fmt == "e4m3":
        words = by_word.astype(ml_dtypes.float8_e4m3fn).view(np.uint8)
    else:
        c = by_word.astype(ml_dtypes.float4_e2m1fn).view(np.uint8) & 0xF
        words = (c[..., 0::2] | (c[..., 1::2] << 4)).reshape(k // 512, 128, 2 * n)
    return np.ascontiguousarray(words), np.ascontiguousarray(byte.astype(np.uint8).reshape(k // 512, 16, n))


def unpack_weight(words, scales, fmt):
    g, _, n = scales.shape
    words = np.ascontiguousarray(words).reshape(g, 128, n, -1)
    if fmt == "e4m3":
        vals = words.view(ml_dtypes.float8_e4m3fn).astype(np.float64)
    else:
        nib = np.empty((g, 128, n, 4), np.uint8)
        nib[..., 0::2] = words & 0xF
        nib[..., 1::2] = words >> 4
        vals = E2M1[nib]
    vals = vals * np.repeat(np.exp2(scales.astype(np.float64) - 127.0), 8, axis=1)[..., None]
    return vals.transpose(0, 1, 3, 2).reshape(g * 512, n)


def gelu(v):
    return 0.5 * v * (1.0 + np.tanh(np.sqrt(2.0 / np.pi) * (v + 0.044715 * v**3)))


K, H, T, S, T3, S2 = 1024, 1536, 2048, 512, 2048, 512

def setup_inputs():
    n = np.random.standard_normal
    s = mx_kscale(K)[:, None]
    u = mx_kscale(H)[:, None]
    tab_words, tab_scales = pack_weight(n((K, T)) * s, "e4m3")
    tab2_words, tab2_scales = pack_weight(n((H, T3)) / np.sqrt(H) / u, "e4m3")
    tab3_words, tab3_scales = pack_weight(n((H, T3)) / np.sqrt(H) / u, "e4m3")
    w1 = (1.3 * n((K, H)) / np.sqrt(K) / s).astype(np.float32)
    w4_words, w4_scales = pack_weight(n((K, H)) / np.sqrt(K) / s, "e2m1")
    return {
        "tab_words": tab_words, "tab_scales": tab_scales,
        "tab2_words": tab2_words, "tab2_scales": tab2_scales,
        "tab3_words": tab3_words, "tab3_scales": tab3_scales,
        "offs": striped(np.random.permutation(T)[:S]),
        "offs2": striped(np.random.permutation(T3)[:S2]),
        "offs3": striped(np.random.permutation(T3)[:S2]),
        "w1": w1, "w4_words": w4_words, "w4_scales": w4_scales,
        "b1": (0.7 * n(H)).astype(np.float32),
        "gain": (np.exp(0.3 * n(H)) * u[:, 0]).astype(np.float32),
        "nav": (0.7 * np.exp(0.3 * n(S2))).astype(np.float32),
    }

def reference(tab_words, tab_scales, tab2_words, tab2_scales, tab3_words, tab3_scales,
              offs, offs2, offs3, w1, w4_words, w4_scales, b1, gain, nav):
    v = unpack_weight(tab_words, tab_scales, "e4m3")[:, unstriped(offs)]
    v2 = unpack_weight(tab2_words, tab2_scales, "e4m3")[:, unstriped(offs2)]
    v3 = unpack_weight(tab3_words, tab3_scales, "e4m3")[:, unstriped(offs3)]
    w4 = unpack_weight(w4_words, w4_scales, "e2m1")
    d = np.tanh((mxq(f64(w1), 0, "e4m3").T @ v) + f64(b1)[:, None])
    h = np.maximum(d, w4.T @ v) * f64(gain)[:, None]
    hq = mxq(h, 0, "e4m3")
    e2 = v2.T @ hq
    e3 = v3.T @ hq
    return np.maximum(e2, e3) + f64(nav)[:, None] * e3

@@ -1,0 +1,232 @@
+from contextlib import ExitStack
+
+import concourse.mybir as mybir
+
+K, H, T, S, S2 = 1024, 1536, 2048, 512, 512
+FLOPS = 2 * 2 * K * H * S + 2 * 2 * H * S2 * S
+
+F32 = mybir.dt.float32
+BF16 = mybir.dt.bfloat16
+I32 = mybir.dt.int32
+U32 = mybir.dt.uint32
+U16 = mybir.dt.uint16
+U8 = mybir.dt.uint8
+FP8X4 = mybir.dt.float8_e4m3fn_x4
+FP4X4 = mybir.dt.float4_e2m1fn_x4
+ACT = mybir.ActivationFunctionType
+ALU = mybir.AluOpType
+
+P = 128
+PACK = 4
+PASS = P * PACK
+KP = K // PASS
+HP = H // PASS
+MT = S2 // P
+CFG = dict(order="L0 b g L2 L1 n c00a c00b ts t0 c01 w4s t1 w0 w1 c10 c11 s3 T30 c20 c21 s2 T31 T32 T2", gain="SSS", il="VVV", cast="SSSSSSSSSSSS", split=2, dbufs=4, lbufs=2, gadd=0, hb=2, z1="010101010101", z4="232323232323", wb=3)
+
+
+def tile_list_rope_team_scores_kernel(
+    tc, tab_words, tab_scales, tab2_words, tab2_scales, tab3_words, tab3_scales,
+    offs, offs2, offs3, w1, w4_words, w4_scales, b1, gain, nav, out,
+):
+    nc = tc.nc
+    with ExitStack() as ctx:
+        keep = ctx.enter_context(tc.tile_pool(name="keep", bufs=1))
+        ring = ctx.enter_context(tc.tile_pool(name="ring", bufs=2))
+        psum = ctx.enter_context(tc.psum_pool(name="psum", bufs=1))
+
+        def held(shape, dtype, name):
+            return keep.tile(shape, dtype, name=name, align_bytes=64)
+
+        lists = [held([P, S // 16], U16, f"list{i}") for i in range(3)]
+        tab_sw = held([P, KP, T], U8, "tab_sw")
+        w4_sraw = held([P, KP, H], U8, "w4_sraw")
+        tab3_sw = held([P, T], U8, "tab3_sw")
+        tab2_sw = held([P, T], U8, "tab2_sw")
+        for plane in (tab_sw, w4_sraw, tab3_sw, tab2_sw):
+            nc.vector.memset(plane[:].bitcast(I32), 0)
+
+        def load_planes_apart(planes, scales):
+            for q in range(4):
+                nc.sync.dma_start(
+                    out=planes[32 * q : 32 * q + 4, :, :].bitcast(I32),
+                    in_=scales[:, 4 * q : 4 * q + 4, :].rearrange("a r t -> r a t").bitcast(I32))
+
+        def load_planes_packed(plane, scales):
+            for q in range(4):
+                nc.sync.dma_start(
+                    out=plane[32 * q + 4 : 32 * q + 4 + 4 * HP, :].bitcast(I32),
+                    in_=scales[:, 4 * q : 4 * q + 4, :].bitcast(I32))
+
+        def load_words(words, a, name):
+            window = held([P, T], I32, name)
+            nc.sync.dma_start(out=window[:], in_=words[a].rearrange("p n i -> p (n i)").bitcast(I32))
+            return window
+
+        HALF = PASS // 2
+
+        def load_w1(b, a, part):
+            rows = w1[PASS * a : PASS * (a + 1), PASS * b : PASS * (b + 1)].rearrange("(p i) c -> p i c", i=PACK)
+            if part == "":
+                raw = held([P, PACK, PASS], F32, f"w1_raw{b}{a}")
+                nc.sync.dma_start(out=raw[:], in_=rows)
+                for u in range(2):
+                    w1_raw[b, a, u] = raw[:, :, HALF * u : HALF * (u + 1)]
+            else:
+                u = "ab".index(part)
+                raw = held([P, PACK, HALF], F32, f"w1_raw{b}{a}{u}")
+                nc.sync.dma_start(out=raw[:], in_=rows[:, :, HALF * u : HALF * (u + 1)])
+                w1_raw[b, a, u] = raw[:]
+
+        w1_raw = {}
+        b1_sb = held([P, HP, PACK], F32, "b1_sb")
+        gain_sb = held([P, HP, PACK], F32, "gain_sb")
+        nav_sb = held([P, MT], F32, "nav_sb")
+        w4_raw = {}
+        tab_w = {}
+        for item in CFG["order"].split():
+            if item[0] == "L":
+                nc.sync.dma_start(lists[int(item[1])][:], (offs, offs2, offs3)[int(item[1])])
+            elif item == "b":
+                nc.sync.dma_start(out=b1_sb[:], in_=b1.rearrange("(b p t) -> p b t", p=P, t=PACK))
+            elif item == "g":
+                nc.sync.dma_start(out=gain_sb[:], in_=gain.rearrange("(b p t) -> p b t", p=P, t=PACK))
+            elif item == "n":
+                with nc.allow_non_contiguous_dma(reason="one value of nav for each partition"):
+                    nc.sync.dma_start(out=nav_sb[:], in_=nav.rearrange("(c p) -> p c", p=P))
+            elif item[0] == "c":
+                load_w1(int(item[1]), int(item[2]), item[3:])
+            elif item == "ts":
+                load_planes_apart(tab_sw, tab_scales)
+            elif item == "w4s":
+                load_planes_apart(w4_sraw, w4_scales)
+            elif item == "s3":
+                load_planes_packed(tab3_sw, tab3_scales)
+            elif item == "s2":
+                load_planes_packed(tab2_sw, tab2_scales)
+            elif item[0] == "w":
+                a = int(item[1])
+                w4_raw[a] = held([P, H // 2], I32, f"w4_raw{a}")
+                nc.sync.dma_start(out=w4_raw[a][:], in_=w4_words[a].bitcast(I32))
+            elif item[0] == "t":
+                tab_w[int(item[1])] = load_words(tab_words, int(item[1]), "tab_w" + item[1])
+            elif item[0] == "T":
+                for a in ([int(item[2])] if len(item) > 2 else range(HP)):
+                    tab_w[item[1], a] = load_words(tab3_words if item[1] == "3" else tab2_words, a, f"tab{item[1]}_w{a}")
+        tab3_w = [tab_w["3", a] for a in range(HP)]
+        tab2_w = [tab_w["2", a] for a in range(HP)]
+
+        def gather(window, offsets, dtype, name):
+            picked = held([P, S], dtype, name)
+            nc.vector.tensor_copy(picked[:], window.indirect(offsets[:]))
+            return picked
+
+        def quantise_w1(b, a):
+            grouped = ring.tile([P, PACK, P, PACK], BF16, name="w1_bf", bufs=CFG["wb"], align_bytes=64)
+            for u in range(2):
+                e = CFG["cast"][2 * (2 * b + a) + u]
+                copy = nc.scalar.copy if e == "S" else nc.vector.tensor_copy
+                copy(out=grouped[:, :, P // 2 * u : P // 2 * (u + 1), :].rearrange("p t m i -> p m i t"),
+                     in_=w1_raw[b, a, u].rearrange("p i (m t) -> p m i t", t=PACK))
+            codes = held([P, PASS], U32, f"w1_codes{b}{a}")
+            scales = held([P, PASS], U8, f"w1_scales{b}{a}")
+            nc.vector.quantize_mx(out=codes[:].bitcast(FP8X4), scales=scales[:],
+                                  in_=grouped[:].rearrange("p t m i -> p (t m i)"))
+            return codes, scales
+
+        def deal_w4(b):
+            words = held([P, KP, PACK, P], U16, f"w4_w{b}")
+            scales = held([P, KP, PACK, P], U8, f"w4_s{b}")
+            cols = slice(PASS * b, PASS * (b + 1))
+            nc.vector.tensor_copy(out=scales[:].rearrange("p a t m -> p a m t"),
+                                  in_=w4_sraw[:, :, cols].rearrange("p a (m t) -> p a m t", t=PACK))
+            for a in range(KP):
+                nc.vector.tensor_copy(out=words[:, a].rearrange("p t (h m) -> p h m t", h=2),
+                                      in_=w4_raw[a][:].bitcast(U16)[:, cols].rearrange("p (h m t) -> p h m t", h=2, t=PACK))
+            return words, scales
+
+        v_s, v_w, w1_q = [], [], {}
+        for a in range(KP):
+            v_s.append(gather(tab_sw[:, a, :], lists[0], U8, f"v_s{a}"))
+            w1_q[0, a] = quantise_w1(0, a)
+            v_w.append(gather(tab_w[a][:].bitcast(U32), lists[0], U32, f"v_w{a}"))
+
+        def features(b):
+            w4_w, w4_s = deal_w4(b)
+            h_rows = ring.tile([P, PACK, S], BF16, name="h_rows", align_bytes=64)
+            for t in range(PACK):
+                cols = slice(P * t, P * (t + 1))
+                z1 = psum.tile([P, S], F32, name="z1", tag="bank" + CFG["z1"][4 * b + t])
+                z4 = psum.tile([P, S], F32, name="z4", tag="bank" + CFG["z4"][4 * b + t])
+                for a in range(KP):
+                    codes, scales = w1_q[b, a]
+                    nc.tensor.matmul_mx(out=z1[:], lhsT=codes[:, cols].bitcast(FP8X4), lhsT_scale=scales[:, cols],
+                                        rhs=v_w[a][:].bitcast(FP8X4), rhs_scale=v_s[a][:],
+                                        start=(a == 0), stop=(a == KP - 1))
+                for a in range(KP):
+                    nc.tensor.matmul_mx(out=z4[:], lhsT=w4_w[:, a, t, :].bitcast(FP4X4),
+                                        lhsT_scale=w4_s[:, a, t, :],
+                                        rhs=v_w[a][:].bitcast(FP8X4), rhs_scale=v_s[a][:],
+                                        start=(a == 0), stop=(a == KP - 1))
+                d = ring.tile([P, S], F32, name="d", tag="first", bufs=CFG["dbufs"], align_bytes=64)
+                nc.scalar.activation(out=d[:], in_=z1[:], func=ACT.Tanh, bias=b1_sb[:, b, t : t + 1])
+                larger = ring.tile([P, S], F32, name="larger", tag="second", bufs=CFG["lbufs"], align_bytes=64)
+                nc.vector.tensor_tensor(out=larger[:], in0=z4[:], in1=d[:], op=ALU.max)
+                if CFG["gain"][b] == "S":
+                    nc.scalar.activation(out=h_rows[:, t, :], in_=larger[:], func=ACT.Copy,
+                                         scale=gain_sb[:, b, t : t + 1])
+                elif CFG["gain"][b] == "V":
+                    nc.vector.tensor_scalar(out=h_rows[:, t, :], in0=larger[:], scalar1=gain_sb[:, b, t : t + 1],
+                                            scalar2=None, op0=ALU.mult)
+                else:
+                    nc.gpsimd.tensor_scalar(out=h_rows[:, t, :], in0=larger[:], scalar1=gain_sb[:, b, t : t + 1],
+                                            scalar2=0.0, op0=ALU.mult, op1=ALU.add)
+            woven = ring.tile([P, S, PACK], BF16, name="woven", align_bytes=64)
+            weave = nc.vector.tensor_copy if CFG["il"][b] == "V" else nc.scalar.copy
+            weave(out=woven[:].rearrange("p (c i) t -> p c t i", i=4),
+                  in_=h_rows[:].rearrange("p t (c i) -> p c t i", i=4))
+            codes = held([P, S], U32, f"h_codes{b}")
+            scales = held([P, S], U8, f"h_scales{b}")
+            nc.vector.quantize_mx(out=codes[:].bitcast(FP8X4), scales=scales[:],
+                                  in_=woven[:].rearrange("p j t -> p (j t)"))
+            return codes, scales
+
+        def score_pass(acc, picked, picked_scales, h_q, b, c):
+            cols = slice(P * c, P * (c + 1))
+            nc.tensor.matmul_mx(out=acc[:], lhsT=picked[:, cols].bitcast(FP8X4),
+                                lhsT_scale=picked_scales[4 * (b + 1) :, cols],
+                                rhs=h_q[0][:].bitcast(FP8X4), rhs_scale=h_q[1][:],
+                                start=(b == 0), stop=(b == HP - 1))
+
+        h_q = [features(0)]
+        for b in range(1, HP):
+            for a in range(KP):
+                w1_q[b, a] = quantise_w1(b, a)
+            h_q.append(features(b))
+
+        v3_s = gather(tab3_sw[:], lists[2], U8, "v3_s")
+        v2_s = gather(tab2_sw[:], lists[1], U8, "v2_s")
+        v3_w = [gather(tab3_w[b][:].bitcast(U32), lists[2], U32, f"v3_w{b}") for b in range(HP)]
+        v2_w = [gather(tab2_w[b][:].bitcast(U32), lists[1], U32, f"v2_w{b}") for b in range(HP)]
+        e3 = [psum.tile([P, S], F32, name=f"e3_{c}", tag=f"bank{4 + c}") for c in range(MT)]
+        e2 = [psum.tile([P, S], F32, name=f"e2_{c}", tag=f"bank{c}") for c in range(MT)]
+        for b in range(HP):
+            for c in range(MT):
+                score_pass(e3[c], v3_w[b], v3_s, h_q[b], b, c)
+        for b in range(HP):
+            for c in range(MT):
+                score_pass(e2[c], v2_w[b], v2_s, h_q[b], b, c)
+        for c in range(MT):
+            e3_sb = ring.tile([P, S], F32, name="e3_sb", tag="first", bufs=CFG["dbufs"], align_bytes=64)
+            nc.scalar.copy(out=e3_sb[:], in_=e3[c][:])
+            larger = ring.tile([P, S], F32, name="larger", tag="second", bufs=CFG["lbufs"], align_bytes=64)
+            nc.vector.tensor_tensor(out=larger[:], in0=e2[c][:], in1=e3_sb[:], op=ALU.max)
+            score = held([P, S], F32, f"score{c}")
+            if c < CFG["gadd"]:
+                scaled = ring.tile([P, S], F32, name="scaled", align_bytes=64)
+                nc.scalar.activation(out=scaled[:], in_=e3[c][:], func=ACT.Copy, scale=nav_sb[:, c : c + 1])
+                nc.gpsimd.tensor_tensor(out=score[:], in0=scaled[:], in1=larger[:], op=ALU.add)
+            else:
+                nc.vector.scalar_tensor_tensor(out=score[:], in0=e3[c][:], scalar=nav_sb[:, c : c + 1], in1=larger[:],
+                                               op0=ALU.mult, op1=ALU.add)
+            nc.sync.dma_start(out=out[P * c : P * (c + 1), :], in_=score[:])

@@ -22,7 +22,8 @@ PASS = P * PACK
 KP = K // PASS
 HP = H // PASS
 MT = S2 // P
-CFG = dict(order="L0 b g L2 L1 n c00a c00b ts t0 c01 w4s t1 w0 w1 c10 c11 s3 T30 c20 c21 s2 T31 T32 T2", gain="SSS", il="VVV", cast="SSSSSSSSSSSS", split=2, dbufs=4, lbufs=2, gadd=0, hb=2, z1="010101010101", z4="232323232323", wb=3)
+HALF = PASS // 2
+CFG = dict(gain="GGS", gadd=1, sq="Y", last="S", w1tag="w1_codes11", vcast="", order="L0 L2 L1 b g ca cb w0 ts t0 c01 w4s t1 w1 s3 c10 w2 s2 c11 c20 T30 c21 T31 T32 n T20 T21 T22", z1="012301230123", z4="456745674567")
 
 
 def tile_list_rope_team_scores_kernel(
@@ -32,19 +33,21 @@ def tile_list_rope_team_scores_kernel(
     nc = tc.nc
     with ExitStack() as ctx:
         keep = ctx.enter_context(tc.tile_pool(name="keep", bufs=1))
-        ring = ctx.enter_context(tc.tile_pool(name="ring", bufs=2))
         psum = ctx.enter_context(tc.psum_pool(name="psum", bufs=1))
 
-        def held(shape, dtype, name):
-            return keep.tile(shape, dtype, name=name, align_bytes=64)
+        def held(shape, dtype, name, tag=None):
+            return keep.tile(shape, dtype, name=name, tag=tag or name, align_bytes=64)
 
         lists = [held([P, S // 16], U16, f"list{i}") for i in range(3)]
         tab_sw = held([P, KP, T], U8, "tab_sw")
         w4_sraw = held([P, KP, H], U8, "w4_sraw")
         tab3_sw = held([P, T], U8, "tab3_sw")
         tab2_sw = held([P, T], U8, "tab2_sw")
-        for plane in (tab_sw, w4_sraw, tab3_sw, tab2_sw):
-            nc.vector.memset(plane[:].bitcast(I32), 0)
+        for plane in (tab_sw, w4_sraw):
+            nc.vector.memset(plane[:, 0, :].bitcast(I32), 0)
+            nc.gpsimd.memset(plane[:, 1, :].bitcast(I32), 0)
+        nc.vector.memset(tab3_sw[:].bitcast(I32), 0)
+        nc.gpsimd.memset(tab2_sw[:].bitcast(I32), 0)
 
         def load_planes_apart(planes, scales):
             for q in range(4):
@@ -54,7 +57,7 @@ def tile_list_rope_team_scores_kernel(
 
         def load_planes_packed(plane, scales):
             for q in range(4):
-                nc.sync.dma_start(
+                (nc.gpsimd if CFG["sq"] == "G" else nc.sync).dma_start(
                     out=plane[32 * q + 4 : 32 * q + 4 + 4 * HP, :].bitcast(I32),
                     in_=scales[:, 4 * q : 4 * q + 4, :].bitcast(I32))
 
@@ -63,27 +66,15 @@ def tile_list_rope_team_scores_kernel(
             nc.sync.dma_start(out=window[:], in_=words[a].rearrange("p n i -> p (n i)").bitcast(I32))
             return window
 
-        HALF = PASS // 2
+        def load_w1(a, cols, name):
+            raw = held([P, PACK, cols.stop - cols.start], F32, name)
+            nc.sync.dma_start(out=raw[:], in_=w1[PASS * a : PASS * (a + 1), cols].rearrange("(p i) c -> p i c", i=PACK))
+            return raw
 
-        def load_w1(b, a, part):
-            rows = w1[PASS * a : PASS * (a + 1), PASS * b : PASS * (b + 1)].rearrange("(p i) c -> p i c", i=PACK)
-            if part == "":
-                raw = held([P, PACK, PASS], F32, f"w1_raw{b}{a}")
-                nc.sync.dma_start(out=raw[:], in_=rows)
-                for u in range(2):
-                    w1_raw[b, a, u] = raw[:, :, HALF * u : HALF * (u + 1)]
-            else:
-                u = "ab".index(part)
-                raw = held([P, PACK, HALF], F32, f"w1_raw{b}{a}{u}")
-                nc.sync.dma_start(out=raw[:], in_=rows[:, :, HALF * u : HALF * (u + 1)])
-                w1_raw[b, a, u] = raw[:]
-
-        w1_raw = {}
+        w1_raw, w4_raw, tab_w = {}, {}, {}
         b1_sb = held([P, HP, PACK], F32, "b1_sb")
         gain_sb = held([P, HP, PACK], F32, "gain_sb")
         nav_sb = held([P, MT], F32, "nav_sb")
-        w4_raw = {}
-        tab_w = {}
         for item in CFG["order"].split():
             if item[0] == "L":
                 nc.sync.dma_start(lists[int(item[1])][:], (offs, offs2, offs3)[int(item[1])])
@@ -94,8 +85,12 @@ def tile_list_rope_team_scores_kernel(
             elif item == "n":
                 with nc.allow_non_contiguous_dma(reason="one value of nav for each partition"):
                     nc.sync.dma_start(out=nav_sb[:], in_=nav.rearrange("(c p) -> p c", p=P))
+            elif item in ("ca", "cb"):
+                u = ("ca", "cb").index(item)
+                w1_raw.setdefault((0, 0), []).append(load_w1(0, slice(HALF * u, HALF * (u + 1)), "w1_raw" + item))
             elif item[0] == "c":
-                load_w1(int(item[1]), int(item[2]), item[3:])
+                b, a = int(item[1]), int(item[2])
+                w1_raw[b, a] = [load_w1(a, slice(PASS * b, PASS * (b + 1)), "w1_raw" + item)]
             elif item == "ts":
                 load_planes_apart(tab_sw, tab_scales)
             elif item == "w4s":
@@ -105,73 +100,86 @@ def tile_list_rope_team_scores_kernel(
             elif item == "s2":
                 load_planes_packed(tab2_sw, tab2_scales)
             elif item[0] == "w":
-                a = int(item[1])
-                w4_raw[a] = held([P, H // 2], I32, f"w4_raw{a}")
-                nc.sync.dma_start(out=w4_raw[a][:], in_=w4_words[a].bitcast(I32))
+                b = int(item[1])
+                w4_raw[b] = held([P, KP, HALF], I32, f"w4_raw{b}")
+                nc.sync.dma_start(out=w4_raw[b][:], in_=w4_words[:, :, 2 * PASS * b : 2 * PASS * (b + 1)].rearrange("a p c -> p a c").bitcast(I32))
             elif item[0] == "t":
                 tab_w[int(item[1])] = load_words(tab_words, int(item[1]), "tab_w" + item[1])
-            elif item[0] == "T":
-                for a in ([int(item[2])] if len(item) > 2 else range(HP)):
-                    tab_w[item[1], a] = load_words(tab3_words if item[1] == "3" else tab2_words, a, f"tab{item[1]}_w{a}")
-        tab3_w = [tab_w["3", a] for a in range(HP)]
-        tab2_w = [tab_w["2", a] for a in range(HP)]
+            else:
+                tab_w[item[1], int(item[2])] = load_words(tab3_words if item[1] == "3" else tab2_words, int(item[2]), item)
 
-        def gather(window, offsets, dtype, name):
-            picked = held([P, S], dtype, name)
+        def gather(window, offsets, dtype, name, tag=None):
+            picked = held([P, S], dtype, name, tag)
             nc.vector.tensor_copy(picked[:], window.indirect(offsets[:]))
             return picked
 
-        def quantise_w1(b, a):
-            grouped = ring.tile([P, PACK, P, PACK], BF16, name="w1_bf", bufs=CFG["wb"], align_bytes=64)
-            for u in range(2):
-                e = CFG["cast"][2 * (2 * b + a) + u]
-                copy = nc.scalar.copy if e == "S" else nc.vector.tensor_copy
-                copy(out=grouped[:, :, P // 2 * u : P // 2 * (u + 1), :].rearrange("p t m i -> p m i t"),
-                     in_=w1_raw[b, a, u].rearrange("p i (m t) -> p m i t", t=PACK))
-            codes = held([P, PASS], U32, f"w1_codes{b}{a}")
+        def quantise_w1(b, a, tag, codes_tag=None):
+            grouped = held([P, PACK, P, PACK], BF16, f"w1_bf{b}{a}", tag)
+            parts = w1_raw[b, a]
+            width = P // len(parts)
+            for u, raw in enumerate(parts):
+                copy = nc.vector.tensor_copy if f"{b}{a}" in CFG["vcast"].split() else nc.scalar.copy
+                copy(out=grouped[:, :, width * u : width * (u + 1), :].rearrange("p t m i -> p m i t"),
+                     in_=raw[:].rearrange("p i (m t) -> p m i t", t=PACK))
+            codes = held([P, PASS], U32, f"w1_codes{b}{a}", codes_tag)
             scales = held([P, PASS], U8, f"w1_scales{b}{a}")
             nc.vector.quantize_mx(out=codes[:].bitcast(FP8X4), scales=scales[:],
                                   in_=grouped[:].rearrange("p t m i -> p (t m i)"))
             return codes, scales
 
-        def deal_w4(b):
-            words = held([P, KP, PACK, P], U16, f"w4_w{b}")
+        def deal_words(b, tag):
+            words = held([P, KP, PACK, P], U16, f"w4_w{b}", tag)
+            nc.vector.tensor_copy(out=words[:].rearrange("p a t m -> p a m t"),
+                                  in_=w4_raw[b][:].bitcast(U16).rearrange("p a (m t) -> p a m t", t=PACK))
+            return words
+
+        def deal_scales(b):
             scales = held([P, KP, PACK, P], U8, f"w4_s{b}")
-            cols = slice(PASS * b, PASS * (b + 1))
             nc.vector.tensor_copy(out=scales[:].rearrange("p a t m -> p a m t"),
-                                  in_=w4_sraw[:, :, cols].rearrange("p a (m t) -> p a m t", t=PACK))
-            for a in range(KP):
-                nc.vector.tensor_copy(out=words[:, a].rearrange("p t (h m) -> p h m t", h=2),
-                                      in_=w4_raw[a][:].bitcast(U16)[:, cols].rearrange("p (h m t) -> p h m t", h=2, t=PACK))
-            return words, scales
+                                  in_=w4_sraw[:, :, PASS * b : PASS * (b + 1)].rearrange("p a (m t) -> p a m t", t=PACK))
+            return scales
 
-        v_s, v_w, w1_q = [], [], {}
-        for a in range(KP):
-            v_s.append(gather(tab_sw[:, a, :], lists[0], U8, f"v_s{a}"))
-            w1_q[0, a] = quantise_w1(0, a)
-            v_w.append(gather(tab_w[a][:].bitcast(U32), lists[0], U32, f"v_w{a}"))
+        w4_w = [deal_words(0, "w4_w0")]
+        w1_q = {(0, 0): quantise_w1(0, 0, "ring0")}
+        v_s = [gather(tab_sw[:, a, :], lists[0], U8, f"v_s{a}") for a in range(KP)]
+        v_w = [gather(tab_w[0][:].bitcast(U32), lists[0], U32, "v_w0")]
+        w4_s = [deal_scales(b) for b in range(HP)]
+        v_w.append(gather(tab_w[1][:].bitcast(U32), lists[0], U32, "v_w1"))
+        w1_q[0, 1] = quantise_w1(0, 1, "ring3")
 
-        def features(b):
-            w4_w, w4_s = deal_w4(b)
-            h_rows = ring.tile([P, PACK, S], BF16, name="h_rows", align_bytes=64)
-            for t in range(PACK):
+        def features(b, first):
+            h_rows = held([P, PACK, S], BF16, f"h_rows{b}", f"h_rows{b % 2}")
+            z1 = [psum.tile([P, S], F32, name=f"z1_{t}", tag="bank" + CFG["z1"][4 * b + t]) for t in range(PACK)]
+            z4 = [psum.tile([P, S], F32, name=f"z4_{t}", tag="bank" + CFG["z4"][4 * b + t]) for t in range(PACK)]
+
+            def sum_w1(t):
                 cols = slice(P * t, P * (t + 1))
-                z1 = psum.tile([P, S], F32, name="z1", tag="bank" + CFG["z1"][4 * b + t])
-                z4 = psum.tile([P, S], F32, name="z4", tag="bank" + CFG["z4"][4 * b + t])
                 for a in range(KP):
                     codes, scales = w1_q[b, a]
-                    nc.tensor.matmul_mx(out=z1[:], lhsT=codes[:, cols].bitcast(FP8X4), lhsT_scale=scales[:, cols],
+                    nc.tensor.matmul_mx(out=z1[t][:], lhsT=codes[:, cols].bitcast(FP8X4), lhsT_scale=scales[:, cols],
                                         rhs=v_w[a][:].bitcast(FP8X4), rhs_scale=v_s[a][:],
                                         start=(a == 0), stop=(a == KP - 1))
+
+            def sum_w4(t):
                 for a in range(KP):
-                    nc.tensor.matmul_mx(out=z4[:], lhsT=w4_w[:, a, t, :].bitcast(FP4X4),
-                                        lhsT_scale=w4_s[:, a, t, :],
+                    nc.tensor.matmul_mx(out=z4[t][:], lhsT=w4_w[b][:, a, t, :].bitcast(FP4X4),
+                                        lhsT_scale=w4_s[b][:, a, t, :],
                                         rhs=v_w[a][:].bitcast(FP8X4), rhs_scale=v_s[a][:],
                                         start=(a == 0), stop=(a == KP - 1))
-                d = ring.tile([P, S], F32, name="d", tag="first", bufs=CFG["dbufs"], align_bytes=64)
-                nc.scalar.activation(out=d[:], in_=z1[:], func=ACT.Tanh, bias=b1_sb[:, b, t : t + 1])
-                larger = ring.tile([P, S], F32, name="larger", tag="second", bufs=CFG["lbufs"], align_bytes=64)
-                nc.vector.tensor_tensor(out=larger[:], in0=z4[:], in1=d[:], op=ALU.max)
+
+            ahead = len(set(CFG["z1"][4 * b : 4 * b + 4]))
+            for t in range(ahead):
+                sum_w1(t)
+            for t in range(ahead):
+                sum_w4(t)
+            for t in range(PACK):
+                if t >= ahead:
+                    sum_w1(t)
+                    sum_w4(t)
+                d = held([P, S], F32, "d", f"ring{(first + t) % 4}")
+                nc.scalar.activation(out=d[:], in_=z1[t][:], func=ACT.Tanh, bias=b1_sb[:, b, t : t + 1])
+                larger = held([P, S], F32, "larger", f"larger{t}")
+                nc.vector.tensor_tensor(out=larger[:], in0=z4[t][:], in1=d[:], op=ALU.max)
                 if CFG["gain"][b] == "S":
                     nc.scalar.activation(out=h_rows[:, t, :], in_=larger[:], func=ACT.Copy,
                                          scale=gain_sb[:, b, t : t + 1])
@@ -181,10 +189,16 @@ def tile_list_rope_team_scores_kernel(
                 else:
                     nc.gpsimd.tensor_scalar(out=h_rows[:, t, :], in0=larger[:], scalar1=gain_sb[:, b, t : t + 1],
                                             scalar2=0.0, op0=ALU.mult, op1=ALU.add)
-            woven = ring.tile([P, S, PACK], BF16, name="woven", align_bytes=64)
-            weave = nc.vector.tensor_copy if CFG["il"][b] == "V" else nc.scalar.copy
-            weave(out=woven[:].rearrange("p (c i) t -> p c t i", i=4),
-                  in_=h_rows[:].rearrange("p t (c i) -> p c t i", i=4))
+            return h_rows
+
+        def weave(h_rows, tag, engine="V"):
+            woven = held([P, S, PACK], BF16, "woven", tag)
+            copy = nc.vector.tensor_copy if engine == "V" else nc.scalar.copy
+            copy(out=woven[:].rearrange("p (c i) t -> p c t i", i=4),
+                 in_=h_rows[:].rearrange("p t (c i) -> p c t i", i=4))
+            return woven
+
+        def quantise_h(b, woven):
             codes = held([P, S], U32, f"h_codes{b}")
             scales = held([P, S], U8, f"h_scales{b}")
             nc.vector.quantize_mx(out=codes[:].bitcast(FP8X4), scales=scales[:],
@@ -198,35 +212,56 @@ def tile_list_rope_team_scores_kernel(
                                 rhs=h_q[0][:].bitcast(FP8X4), rhs_scale=h_q[1][:],
                                 start=(b == 0), stop=(b == HP - 1))
 
-        h_q = [features(0)]
-        for b in range(1, HP):
-            for a in range(KP):
-                w1_q[b, a] = quantise_w1(b, a)
-            h_q.append(features(b))
+        def pick3(b):
+            return gather(tab_w["3", b][:].bitcast(U32), lists[2], U32, f"v3_w{b}")
 
+        def pick2(b):
+            return gather(tab_w["2", b][:].bitcast(U32), lists[1], U32, f"v2_w{b}")
+
+        w4_w.append(deal_words(1, "w4_w1"))
         v3_s = gather(tab3_sw[:], lists[2], U8, "v3_s")
+        h_rows = features(0, 0)
+        w4_w.append(deal_words(2, "w4_w0"))
         v2_s = gather(tab2_sw[:], lists[1], U8, "v2_s")
-        v3_w = [gather(tab3_w[b][:].bitcast(U32), lists[2], U32, f"v3_w{b}") for b in range(HP)]
-        v2_w = [gather(tab2_w[b][:].bitcast(U32), lists[1], U32, f"v2_w{b}") for b in range(HP)]
+        w1_q[1, 0] = quantise_w1(1, 0, "w1_codes01")
+        w1_q[1, 1] = quantise_w1(1, 1, "ring1")
+        h_q = [quantise_h(0, weave(h_rows, "woven"))]
+        v3_w = [pick3(0)]
+        w1_q[2, 0] = quantise_w1(2, 0, "ring2", "T30")
+        h_rows = features(1, 3)
+        v3_w.append(pick3(1))
+        w1_q[2, 1] = quantise_w1(2, 1, "w1_codes11")
+        h_q.append(quantise_h(1, weave(h_rows, CFG["w1tag"])))
+        h_rows = features(2, 0)
+        v3_w.append(pick3(2))
+        v2_w = [pick2(0)]
+        v2_w.append(pick2(1))
+        if CFG["last"] == "V":
+            h_q.append(quantise_h(2, weave(h_rows, "T21")))
+            v2_w.append(pick2(2))
+        else:
+            v2_w.append(pick2(2))
+            h_q.append(quantise_h(2, weave(h_rows, "woven", "S")))
         e3 = [psum.tile([P, S], F32, name=f"e3_{c}", tag=f"bank{4 + c}") for c in range(MT)]
         e2 = [psum.tile([P, S], F32, name=f"e2_{c}", tag=f"bank{c}") for c in range(MT)]
         for b in range(HP):
             for c in range(MT):
                 score_pass(e3[c], v3_w[b], v3_s, h_q[b], b, c)
-        for b in range(HP):
-            for c in range(MT):
                 score_pass(e2[c], v2_w[b], v2_s, h_q[b], b, c)
+        larger, score = [], []
         for c in range(MT):
-            e3_sb = ring.tile([P, S], F32, name="e3_sb", tag="first", bufs=CFG["dbufs"], align_bytes=64)
+            e3_sb = held([P, S], F32, "e3_sb", f"ring{c}")
             nc.scalar.copy(out=e3_sb[:], in_=e3[c][:])
-            larger = ring.tile([P, S], F32, name="larger", tag="second", bufs=CFG["lbufs"], align_bytes=64)
-            nc.vector.tensor_tensor(out=larger[:], in0=e2[c][:], in1=e3_sb[:], op=ALU.max)
-            score = held([P, S], F32, f"score{c}")
+            larger.append(held([P, S], F32, "larger", f"larger{c}"))
+            nc.vector.tensor_tensor(out=larger[c][:], in0=e2[c][:], in1=e3_sb[:], op=ALU.max)
+            score.append(held([P, S], F32, f"score{c}"))
             if c < CFG["gadd"]:
-                scaled = ring.tile([P, S], F32, name="scaled", align_bytes=64)
-                nc.scalar.activation(out=scaled[:], in_=e3[c][:], func=ACT.Copy, scale=nav_sb[:, c : c + 1])
-                nc.gpsimd.tensor_tensor(out=score[:], in0=scaled[:], in1=larger[:], op=ALU.add)
-            else:
-                nc.vector.scalar_tensor_tensor(out=score[:], in0=e3[c][:], scalar=nav_sb[:, c : c + 1], in1=larger[:],
+                scaled = held([P, S], F32, f"scaled{c}", f"h_rows{c}")
+                nc.gpsimd.tensor_scalar(out=scaled[:], in0=e3_sb[:], scalar1=nav_sb[:, c : c + 1], scalar2=0.0,
+                                        op0=ALU.mult, op1=ALU.add)
+                nc.gpsimd.tensor_tensor(out=score[c][:], in0=scaled[:], in1=larger[c][:], op=ALU.add)
+        for c in range(MT):
+            if c >= CFG["gadd"]:
+                nc.vector.scalar_tensor_tensor(out=score[c][:], in0=e3[c][:], scalar=nav_sb[:, c : c + 1], in1=larger[c][:],
                                                op0=ALU.mult, op1=ALU.add)
-            nc.sync.dma_start(out=out[P * c : P * (c + 1), :], in_=score[:])
+            nc.sync.dma_start(out=out[P * c : P * (c + 1), :], in_=score[c][:])

@@ -23,7 +23,7 @@ KP = K // PASS
 HP = H // PASS
 MT = S2 // P
 HALF = PASS // 2
-CFG = dict(gain="GGS", gadd=1, sq="Y", last="S", w1tag="w1_codes11", vcast="", order="L0 L2 L1 b g ca cb w0 ts t0 c01 w4s t1 w1 s3 c10 w2 s2 c11 c20 T30 c21 T31 T32 n T20 T21 T22", z1="012301230123", z4="456745674567")
+CFG = dict(gain="GGG", gadd=1, sq="YY", il="SS", early=1, il0="V", tie="h1:T20 h2:T32 w0:w1_rawc11", m20="T20", h1="h1", t3="a b e", t2="f c d", w1tag="w1_codes11", vcast="21 x", order="L0 L2 L1 w0 w1 w2 ca cb ts t0 c01 w4s t1 b s3 g c10 c11 s2 c20 c21 T30 T31 T20 n T21 T32 T22", z1="012301230123", z4="456745674567")
 
 
 def tile_list_rope_team_scores_kernel(
@@ -55,9 +55,9 @@ def tile_list_rope_team_scores_kernel(
                     out=planes[32 * q : 32 * q + 4, :, :].bitcast(I32),
                     in_=scales[:, 4 * q : 4 * q + 4, :].rearrange("a r t -> r a t").bitcast(I32))
 
-        def load_planes_packed(plane, scales):
+        def load_planes_packed(plane, scales, queue):
             for q in range(4):
-                (nc.gpsimd if CFG["sq"] == "G" else nc.sync).dma_start(
+                (nc.gpsimd if queue == "G" else nc.sync).dma_start(
                     out=plane[32 * q + 4 : 32 * q + 4 + 4 * HP, :].bitcast(I32),
                     in_=scales[:, 4 * q : 4 * q + 4, :].bitcast(I32))
 
@@ -72,16 +72,16 @@ def tile_list_rope_team_scores_kernel(
             return raw
 
         w1_raw, w4_raw, tab_w = {}, {}, {}
-        b1_sb = held([P, HP, PACK], F32, "b1_sb")
-        gain_sb = held([P, HP, PACK], F32, "gain_sb")
+        b1_sb = held([P, HP, 2 * PACK], F32, "b1_sb")
+        gain_sb = held([P, HP, 2 * PACK], F32, "gain_sb")
         nav_sb = held([P, MT], F32, "nav_sb")
         for item in CFG["order"].split():
             if item[0] == "L":
                 nc.sync.dma_start(lists[int(item[1])][:], (offs, offs2, offs3)[int(item[1])])
             elif item == "b":
-                nc.sync.dma_start(out=b1_sb[:], in_=b1.rearrange("(b p t) -> p b t", p=P, t=PACK))
+                nc.sync.dma_start(out=b1_sb[:, :, 0:PACK], in_=b1.rearrange("(b p t) -> p b t", p=P, t=PACK))
             elif item == "g":
-                nc.sync.dma_start(out=gain_sb[:], in_=gain.rearrange("(b p t) -> p b t", p=P, t=PACK))
+                nc.sync.dma_start(out=gain_sb[:, :, 0:PACK], in_=gain.rearrange("(b p t) -> p b t", p=P, t=PACK))
             elif item == "n":
                 with nc.allow_non_contiguous_dma(reason="one value of nav for each partition"):
                     nc.sync.dma_start(out=nav_sb[:], in_=nav.rearrange("(c p) -> p c", p=P))
@@ -96,9 +96,9 @@ def tile_list_rope_team_scores_kernel(
             elif item == "w4s":
                 load_planes_apart(w4_sraw, w4_scales)
             elif item == "s3":
-                load_planes_packed(tab3_sw, tab3_scales)
+                load_planes_packed(tab3_sw, tab3_scales, CFG["sq"][0])
             elif item == "s2":
-                load_planes_packed(tab2_sw, tab2_scales)
+                load_planes_packed(tab2_sw, tab2_scales, CFG["sq"][1])
             elif item[0] == "w":
                 b = int(item[1])
                 w4_raw[b] = held([P, KP, HALF], I32, f"w4_raw{b}")
@@ -139,7 +139,7 @@ def tile_list_rope_team_scores_kernel(
                                   in_=w4_sraw[:, :, PASS * b : PASS * (b + 1)].rearrange("p a (m t) -> p a m t", t=PACK))
             return scales
 
-        w4_w = [deal_words(0, "w4_w0")]
+        w4_w = [deal_words(b, f"w4_w{b}") for b in range(HP if CFG["early"] else 1)]
         w1_q = {(0, 0): quantise_w1(0, 0, "ring0")}
         v_s = [gather(tab_sw[:, a, :], lists[0], U8, f"v_s{a}") for a in range(KP)]
         v_w = [gather(tab_w[0][:].bitcast(U32), lists[0], U32, "v_w0")]
@@ -178,7 +178,7 @@ def tile_list_rope_team_scores_kernel(
                     sum_w4(t)
                 d = held([P, S], F32, "d", f"ring{(first + t) % 4}")
                 nc.scalar.activation(out=d[:], in_=z1[t][:], func=ACT.Tanh, bias=b1_sb[:, b, t : t + 1])
-                larger = held([P, S], F32, "larger", f"larger{t}")
+                larger = held([P, S], F32, "larger", tie.get(f"m{b}{t}", f"larger{t}"))
                 nc.vector.tensor_tensor(out=larger[:], in0=z4[t][:], in1=d[:], op=ALU.max)
                 if CFG["gain"][b] == "S":
                     nc.scalar.activation(out=h_rows[:, t, :], in_=larger[:], func=ACT.Copy,
@@ -198,8 +198,8 @@ def tile_list_rope_team_scores_kernel(
                  in_=h_rows[:].rearrange("p t (c i) -> p c t i", i=4))
             return woven
 
-        def quantise_h(b, woven):
-            codes = held([P, S], U32, f"h_codes{b}")
+        def quantise_h(b, woven, tag):
+            codes = held([P, S], U32, f"h_codes{b}", tag)
             scales = held([P, S], U8, f"h_scales{b}")
             nc.vector.quantize_mx(out=codes[:].bitcast(FP8X4), scales=scales[:],
                                   in_=woven[:].rearrange("p j t -> p (j t)"))
@@ -213,46 +213,46 @@ def tile_list_rope_team_scores_kernel(
                                 start=(b == 0), stop=(b == HP - 1))
 
         def pick3(b):
-            return gather(tab_w["3", b][:].bitcast(U32), lists[2], U32, f"v3_w{b}")
+            return gather(tab_w["3", b][:].bitcast(U32), lists[2], U32, f"v3_w{b}", CFG["t3"].split()[b])
 
         def pick2(b):
-            return gather(tab_w["2", b][:].bitcast(U32), lists[1], U32, f"v2_w{b}")
+            return gather(tab_w["2", b][:].bitcast(U32), lists[1], U32, f"v2_w{b}", CFG["t2"].split()[b])
 
-        w4_w.append(deal_words(1, "w4_w1"))
+        tie = dict(pair.split(":") for pair in CFG["tie"].split())
+        if CFG["early"] == 0:
+            w4_w.append(deal_words(1, "w4_w1"))
         v3_s = gather(tab3_sw[:], lists[2], U8, "v3_s")
-        h_rows = features(0, 0)
-        w4_w.append(deal_words(2, "w4_w0"))
-        v2_s = gather(tab2_sw[:], lists[1], U8, "v2_s")
+        rows0 = features(0, 0)
+        if CFG["early"] == 0:
+            w4_w.append(deal_words(2, "w4_w0"))
         w1_q[1, 0] = quantise_w1(1, 0, "w1_codes01")
         w1_q[1, 1] = quantise_w1(1, 1, "ring1")
-        h_q = [quantise_h(0, weave(h_rows, "woven"))]
+        h_q = [quantise_h(0, weave(rows0, tie.get("w0", "woven0"), CFG["il0"]), None)]
+        v2_s = gather(tab2_sw[:], lists[1], U8, "v2_s")
+        w1_q[2, 0] = quantise_w1(2, 0, "ring2")
+        w1_q[2, 1] = quantise_w1(2, 1, "w1_codes01")
         v3_w = [pick3(0)]
-        w1_q[2, 0] = quantise_w1(2, 0, "ring2", "T30")
-        h_rows = features(1, 3)
+        rows1 = features(1, 3)
         v3_w.append(pick3(1))
-        w1_q[2, 1] = quantise_w1(2, 1, "w1_codes11")
-        h_q.append(quantise_h(1, weave(h_rows, CFG["w1tag"])))
-        h_rows = features(2, 0)
-        v3_w.append(pick3(2))
+        rows2 = features(2, 3)
         v2_w = [pick2(0)]
+        h_q.append(quantise_h(1, weave(rows1, "woven1", CFG["il"][0]), tie.get("h1")))
         v2_w.append(pick2(1))
-        if CFG["last"] == "V":
-            h_q.append(quantise_h(2, weave(h_rows, "T21")))
-            v2_w.append(pick2(2))
-        else:
-            v2_w.append(pick2(2))
-            h_q.append(quantise_h(2, weave(h_rows, "woven", "S")))
+        v3_w.append(pick3(2))
+        h_q.append(quantise_h(2, weave(rows2, tie.get("w2", "woven0"), CFG["il"][1]), tie.get("h2")))
+        v2_w.append(pick2(2))
         e3 = [psum.tile([P, S], F32, name=f"e3_{c}", tag=f"bank{4 + c}") for c in range(MT)]
         e2 = [psum.tile([P, S], F32, name=f"e2_{c}", tag=f"bank{c}") for c in range(MT)]
         for b in range(HP):
             for c in range(MT):
                 score_pass(e3[c], v3_w[b], v3_s, h_q[b], b, c)
+            for c in range(MT):
                 score_pass(e2[c], v2_w[b], v2_s, h_q[b], b, c)
         larger, score = [], []
         for c in range(MT):
-            e3_sb = held([P, S], F32, "e3_sb", f"ring{c}")
+            e3_sb = held([P, S], F32, "e3_sb", f"ring{(c + 3) % 4}")
             nc.scalar.copy(out=e3_sb[:], in_=e3[c][:])
-            larger.append(held([P, S], F32, "larger", f"larger{c}"))
+            larger.append(held([P, S], F32, "larger", f"final{c}"))
             nc.vector.tensor_tensor(out=larger[c][:], in0=e2[c][:], in1=e3_sb[:], op=ALU.max)
             score.append(held([P, S], F32, f"score{c}"))
             if c < CFG["gadd"]:

@@ -23,7 +23,7 @@ KP = K // PASS
 HP = H // PASS
 MT = S2 // P
 HALF = PASS // 2
-CFG = dict(gain="GGG", gadd=1, sq="YY", il="SS", early=1, il0="V", tie="h1:T20 h2:T32 w0:w1_rawc11", m20="T20", h1="h1", t3="a b e", t2="f c d", w1tag="w1_codes11", vcast="21 x", order="L0 L2 L1 w0 w1 w2 ca cb ts t0 c01 w4s t1 b s3 g c10 c11 s2 c20 c21 T30 T31 T20 n T21 T32 T22", z1="012301230123", z4="456745674567")
+CFG = dict(gain="GGG", gadd=1, sq="YY", il="SS", early=0, w4q="Y", il0="V", tie="h1:T20 h2:T32 w0:w1_rawc11", m20="T20", h1="h1", t3="a b e", t2="f c d", w1tag="w1_codes11", vcast="21 x", order="L0 L2 L1 w0 da db ts t0 c01 w4s t1 b w1 s3 g c10 w2 c11 s2 c20 c21 T30 T31 T20 n T21 T32 T22", z1="012301230123", z4="456745674567")
 
 
 def tile_list_rope_team_scores_kernel(
@@ -49,9 +49,9 @@ def tile_list_rope_team_scores_kernel(
         nc.vector.memset(tab3_sw[:].bitcast(I32), 0)
         nc.gpsimd.memset(tab2_sw[:].bitcast(I32), 0)
 
-        def load_planes_apart(planes, scales):
+        def load_planes_apart(planes, scales, queue):
             for q in range(4):
-                nc.sync.dma_start(
+                queue.dma_start(
                     out=planes[32 * q : 32 * q + 4, :, :].bitcast(I32),
                     in_=scales[:, 4 * q : 4 * q + 4, :].rearrange("a r t -> r a t").bitcast(I32))
 
@@ -88,13 +88,20 @@ def tile_list_rope_team_scores_kernel(
             elif item in ("ca", "cb"):
                 u = ("ca", "cb").index(item)
                 w1_raw.setdefault((0, 0), []).append(load_w1(0, slice(HALF * u, HALF * (u + 1)), "w1_raw" + item))
+            elif item in ("da", "db"):
+                u = ("da", "db").index(item)
+                raw = held([P, PACK, HALF], F32, "w1_raw" + item)
+                rows = w1[0:PASS, HALF * u : HALF * (u + 1)].rearrange("(p i) c -> p i c", i=PACK)
+                for i in range(0, PACK, 2):
+                    nc.sync.dma_start(out=raw[:, i : i + 2, :], in_=rows[:, i : i + 2, :])
+                w1_raw.setdefault((0, 0), []).append(raw)
             elif item[0] == "c":
                 b, a = int(item[1]), int(item[2])
                 w1_raw[b, a] = [load_w1(a, slice(PASS * b, PASS * (b + 1)), "w1_raw" + item)]
             elif item == "ts":
-                load_planes_apart(tab_sw, tab_scales)
+                load_planes_apart(tab_sw, tab_scales, nc.sync)
             elif item == "w4s":
-                load_planes_apart(w4_sraw, w4_scales)
+                load_planes_apart(w4_sraw, w4_scales, nc.gpsimd if CFG["w4q"] == "G" else nc.sync)
             elif item == "s3":
                 load_planes_packed(tab3_sw, tab3_scales, CFG["sq"][0])
             elif item == "s2":
@@ -119,8 +126,8 @@ def tile_list_rope_team_scores_kernel(
             width = P // len(parts)
             for u, raw in enumerate(parts):
                 copy = nc.vector.tensor_copy if f"{b}{a}" in CFG["vcast"].split() else nc.scalar.copy
-                copy(out=grouped[:, :, width * u : width * (u + 1), :].rearrange("p t m i -> p m i t"),
-                     in_=raw[:].rearrange("p i (m t) -> p m i t", t=PACK))
+                copy(out=grouped[:, :, width * u : width * (u + 1), :].rearrange("p (h e) m i -> p h m i e", e=2),
+                     in_=raw[:].rearrange("p i (m h e) -> p h m i e", h=2, e=2))
             codes = held([P, PASS], U32, f"w1_codes{b}{a}", codes_tag)
             scales = held([P, PASS], U8, f"w1_scales{b}{a}")
             nc.vector.quantize_mx(out=codes[:].bitcast(FP8X4), scales=scales[:],
@@ -129,14 +136,14 @@ def tile_list_rope_team_scores_kernel(
 
         def deal_words(b, tag):
             words = held([P, KP, PACK, P], U16, f"w4_w{b}", tag)
-            nc.vector.tensor_copy(out=words[:].rearrange("p a t m -> p a m t"),
-                                  in_=w4_raw[b][:].bitcast(U16).rearrange("p a (m t) -> p a m t", t=PACK))
+            nc.vector.tensor_copy(out=words[:].rearrange("p a (h e) m -> p a h m e", e=2),
+                                  in_=w4_raw[b][:].bitcast(U16).rearrange("p a (m h e) -> p a h m e", h=2, e=2))
             return words
 
         def deal_scales(b):
             scales = held([P, KP, PACK, P], U8, f"w4_s{b}")
-            nc.vector.tensor_copy(out=scales[:].rearrange("p a t m -> p a m t"),
-                                  in_=w4_sraw[:, :, PASS * b : PASS * (b + 1)].rearrange("p a (m t) -> p a m t", t=PACK))
+            nc.vector.tensor_copy(out=scales[:].rearrange("p a (h e) m -> p a h m e", e=2),
+                                  in_=w4_sraw[:, :, PASS * b : PASS * (b + 1)].rearrange("p a (m h e) -> p a h m e", h=2, e=2))
             return scales
 
         w4_w = [deal_words(b, f"w4_w{b}") for b in range(HP if CFG["early"] else 1)]

from contextlib import ExitStack

import concourse.mybir as mybir

K, H, T, S, S2 = 1024, 1536, 2048, 512, 512
FLOPS = 2 * 2 * K * H * S + 2 * 2 * H * S2 * S

F32 = mybir.dt.float32
BF16 = mybir.dt.bfloat16
I32 = mybir.dt.int32
U32 = mybir.dt.uint32
U16 = mybir.dt.uint16
U8 = mybir.dt.uint8
FP8X4 = mybir.dt.float8_e4m3fn_x4
FP4X4 = mybir.dt.float4_e2m1fn_x4
ACT = mybir.ActivationFunctionType
ALU = mybir.AluOpType

P = 128
PACK = 4
PASS = P * PACK
KP = K // PASS
HP = H // PASS
MT = S2 // P
HALF = PASS // 2
CFG = dict(gain="GGG", gadd=1, sq="YY", il="SS", early=0, w4q="Y", il0="V", tie="h1:T20 h2:T32 w0:w1_rawc11", m20="T20", h1="h1", t3="a b e", t2="f c d", w1tag="w1_codes11", vcast="21 x", order="L0 L2 L1 w0 da db ts t0 c01 w4s t1 b w1 s3 g c10 w2 c11 s2 c20 c21 T30 T31 T20 n T21 T32 T22", z1="012301230123", z4="456745674567")


def tile_list_rope_team_scores_kernel(
    tc, tab_words, tab_scales, tab2_words, tab2_scales, tab3_words, tab3_scales,
    offs, offs2, offs3, w1, w4_words, w4_scales, b1, gain, nav, out,
):
    nc = tc.nc
    with ExitStack() as ctx:
        keep = ctx.enter_context(tc.tile_pool(name="keep", bufs=1))
        psum = ctx.enter_context(tc.psum_pool(name="psum", bufs=1))

        def held(shape, dtype, name, tag=None):
            return keep.tile(shape, dtype, name=name, tag=tag or name, align_bytes=64)

        lists = [held([P, S // 16], U16, f"list{i}") for i in range(3)]
        tab_sw = held([P, KP, T], U8, "tab_sw")
        w4_sraw = held([P, KP, H], U8, "w4_sraw")
        tab3_sw = held([P, T], U8, "tab3_sw")
        tab2_sw = held([P, T], U8, "tab2_sw")
        for plane in (tab_sw, w4_sraw):
            nc.vector.memset(plane[:, 0, :].bitcast(I32), 0)
            nc.gpsimd.memset(plane[:, 1, :].bitcast(I32), 0)
        nc.vector.memset(tab3_sw[:].bitcast(I32), 0)
        nc.gpsimd.memset(tab2_sw[:].bitcast(I32), 0)

        def load_planes_apart(planes, scales, queue):
            for q in range(4):
                queue.dma_start(
                    out=planes[32 * q : 32 * q + 4, :, :].bitcast(I32),
                    in_=scales[:, 4 * q : 4 * q + 4, :].rearrange("a r t -> r a t").bitcast(I32))

        def load_planes_packed(plane, scales, queue):
            for q in range(4):
                (nc.gpsimd if queue == "G" else nc.sync).dma_start(
                    out=plane[32 * q + 4 : 32 * q + 4 + 4 * HP, :].bitcast(I32),
                    in_=scales[:, 4 * q : 4 * q + 4, :].bitcast(I32))

        def load_words(words, a, name):
            window = held([P, T], I32, name)
            nc.sync.dma_start(out=window[:], in_=words[a].rearrange("p n i -> p (n i)").bitcast(I32))
            return window

        def load_w1(a, cols, name):
            raw = held([P, PACK, cols.stop - cols.start], F32, name)
            nc.sync.dma_start(out=raw[:], in_=w1[PASS * a : PASS * (a + 1), cols].rearrange("(p i) c -> p i c", i=PACK))
            return raw

        w1_raw, w4_raw, tab_w = {}, {}, {}
        b1_sb = held([P, HP, 2 * PACK], F32, "b1_sb")
        gain_sb = held([P, HP, 2 * PACK], F32, "gain_sb")
        nav_sb = held([P, MT], F32, "nav_sb")
        for item in CFG["order"].split():
            if item[0] == "L":
                nc.sync.dma_start(lists[int(item[1])][:], (offs, offs2, offs3)[int(item[1])])
            elif item == "b":
                nc.sync.dma_start(out=b1_sb[:, :, 0:PACK], in_=b1.rearrange("(b p t) -> p b t", p=P, t=PACK))
            elif item == "g":
                nc.sync.dma_start(out=gain_sb[:, :, 0:PACK], in_=gain.rearrange("(b p t) -> p b t", p=P, t=PACK))
            elif item == "n":
                with nc.allow_non_contiguous_dma(reason="one value of nav for each partition"):
                    nc.sync.dma_start(out=nav_sb[:], in_=nav.rearrange("(c p) -> p c", p=P))
            elif item in ("ca", "cb"):
                u = ("ca", "cb").index(item)
                w1_raw.setdefault((0, 0), []).append(load_w1(0, slice(HALF * u, HALF * (u + 1)), "w1_raw" + item))
            elif item in ("da", "db"):
                u = ("da", "db").index(item)
                raw = held([P, PACK, HALF], F32, "w1_raw" + item)
                rows = w1[0:PASS, HALF * u : HALF * (u + 1)].rearrange("(p i) c -> p i c", i=PACK)
                for i in range(0, PACK, 2):
                    nc.sync.dma_start(out=raw[:, i : i + 2, :], in_=rows[:, i : i + 2, :])
                w1_raw.setdefault((0, 0), []).append(raw)
            elif item[0] == "c":
                b, a = int(item[1]), int(item[2])
                w1_raw[b, a] = [load_w1(a, slice(PASS * b, PASS * (b + 1)), "w1_raw" + item)]
            elif item == "ts":
                load_planes_apart(tab_sw, tab_scales, nc.sync)
            elif item == "w4s":
                load_planes_apart(w4_sraw, w4_scales, nc.gpsimd if CFG["w4q"] == "G" else nc.sync)
            elif item == "s3":
                load_planes_packed(tab3_sw, tab3_scales, CFG["sq"][0])
            elif item == "s2":
                load_planes_packed(tab2_sw, tab2_scales, CFG["sq"][1])
            elif item[0] == "w":
                b = int(item[1])
                w4_raw[b] = held([P, KP, HALF], I32, f"w4_raw{b}")
                nc.sync.dma_start(out=w4_raw[b][:], in_=w4_words[:, :, 2 * PASS * b : 2 * PASS * (b + 1)].rearrange("a p c -> p a c").bitcast(I32))
            elif item[0] == "t":
                tab_w[int(item[1])] = load_words(tab_words, int(item[1]), "tab_w" + item[1])
            else:
                tab_w[item[1], int(item[2])] = load_words(tab3_words if item[1] == "3" else tab2_words, int(item[2]), item)

        def gather(window, offsets, dtype, name, tag=None):
            picked = held([P, S], dtype, name, tag)
            nc.vector.tensor_copy(picked[:], window.indirect(offsets[:]))
            return picked

        def quantise_w1(b, a, tag, codes_tag=None):
            grouped = held([P, PACK, P, PACK], BF16, f"w1_bf{b}{a}", tag)
            parts = w1_raw[b, a]
            width = P // len(parts)
            for u, raw in enumerate(parts):
                copy = nc.vector.tensor_copy if f"{b}{a}" in CFG["vcast"].split() else nc.scalar.copy
                copy(out=grouped[:, :, width * u : width * (u + 1), :].rearrange("p (h e) m i -> p h m i e", e=2),
                     in_=raw[:].rearrange("p i (m h e) -> p h m i e", h=2, e=2))
            codes = held([P, PASS], U32, f"w1_codes{b}{a}", codes_tag)
            scales = held([P, PASS], U8, f"w1_scales{b}{a}")
            nc.vector.quantize_mx(out=codes[:].bitcast(FP8X4), scales=scales[:],
                                  in_=grouped[:].rearrange("p t m i -> p (t m i)"))
            return codes, scales

        def deal_words(b, tag):
            words = held([P, KP, PACK, P], U16, f"w4_w{b}", tag)
            nc.vector.tensor_copy(out=words[:].rearrange("p a (h e) m -> p a h m e", e=2),
                                  in_=w4_raw[b][:].bitcast(U16).rearrange("p a (m h e) -> p a h m e", h=2, e=2))
            return words

        def deal_scales(b):
            scales = held([P, KP, PACK, P], U8, f"w4_s{b}")
            nc.vector.tensor_copy(out=scales[:].rearrange("p a (h e) m -> p a h m e", e=2),
                                  in_=w4_sraw[:, :, PASS * b : PASS * (b + 1)].rearrange("p a (m h e) -> p a h m e", h=2, e=2))
            return scales

        w4_w = [deal_words(b, f"w4_w{b}") for b in range(HP if CFG["early"] else 1)]
        w1_q = {(0, 0): quantise_w1(0, 0, "ring0")}
        v_s = [gather(tab_sw[:, a, :], lists[0], U8, f"v_s{a}") for a in range(KP)]
        v_w = [gather(tab_w[0][:].bitcast(U32), lists[0], U32, "v_w0")]
        w4_s = [deal_scales(b) for b in range(HP)]
        v_w.append(gather(tab_w[1][:].bitcast(U32), lists[0], U32, "v_w1"))
        w1_q[0, 1] = quantise_w1(0, 1, "ring3")

        def features(b, first):
            h_rows = held([P, PACK, S], BF16, f"h_rows{b}", f"h_rows{b % 2}")
            z1 = [psum.tile([P, S], F32, name=f"z1_{t}", tag="bank" + CFG["z1"][4 * b + t]) for t in range(PACK)]
            z4 = [psum.tile([P, S], F32, name=f"z4_{t}", tag="bank" + CFG["z4"][4 * b + t]) for t in range(PACK)]

            def sum_w1(t):
                cols = slice(P * t, P * (t + 1))
                for a in range(KP):
                    codes, scales = w1_q[b, a]
                    nc.tensor.matmul_mx(out=z1[t][:], lhsT=codes[:, cols].bitcast(FP8X4), lhsT_scale=scales[:, cols],
                                        rhs=v_w[a][:].bitcast(FP8X4), rhs_scale=v_s[a][:],
                                        start=(a == 0), stop=(a == KP - 1))

            def sum_w4(t):
                for a in range(KP):
                    nc.tensor.matmul_mx(out=z4[t][:], lhsT=w4_w[b][:, a, t, :].bitcast(FP4X4),
                                        lhsT_scale=w4_s[b][:, a, t, :],
                                        rhs=v_w[a][:].bitcast(FP8X4), rhs_scale=v_s[a][:],
                                        start=(a == 0), stop=(a == KP - 1))

            ahead = len(set(CFG["z1"][4 * b : 4 * b + 4]))
            for t in range(ahead):
                sum_w1(t)
            for t in range(ahead):
                sum_w4(t)
            for t in range(PACK):
                if t >= ahead:
                    sum_w1(t)
                    sum_w4(t)
                d = held([P, S], F32, "d", f"ring{(first + t) % 4}")
                nc.scalar.activation(out=d[:], in_=z1[t][:], func=ACT.Tanh, bias=b1_sb[:, b, t : t + 1])
                larger = held([P, S], F32, "larger", tie.get(f"m{b}{t}", f"larger{t}"))
                nc.vector.tensor_tensor(out=larger[:], in0=z4[t][:], in1=d[:], op=ALU.max)
                if CFG["gain"][b] == "S":
                    nc.scalar.activation(out=h_rows[:, t, :], in_=larger[:], func=ACT.Copy,
                                         scale=gain_sb[:, b, t : t + 1])
                elif CFG["gain"][b] == "V":
                    nc.vector.tensor_scalar(out=h_rows[:, t, :], in0=larger[:], scalar1=gain_sb[:, b, t : t + 1],
                                            scalar2=None, op0=ALU.mult)
                else:
                    nc.gpsimd.tensor_scalar(out=h_rows[:, t, :], in0=larger[:], scalar1=gain_sb[:, b, t : t + 1],
                                            scalar2=0.0, op0=ALU.mult, op1=ALU.add)
            return h_rows

        def weave(h_rows, tag, engine="V"):
            woven = held([P, S, PACK], BF16, "woven", tag)
            copy = nc.vector.tensor_copy if engine == "V" else nc.scalar.copy
            copy(out=woven[:].rearrange("p (c i) t -> p c t i", i=4),
                 in_=h_rows[:].rearrange("p t (c i) -> p c t i", i=4))
            return woven

        def quantise_h(b, woven, tag):
            codes = held([P, S], U32, f"h_codes{b}", tag)
            scales = held([P, S], U8, f"h_scales{b}")
            nc.vector.quantize_mx(out=codes[:].bitcast(FP8X4), scales=scales[:],
                                  in_=woven[:].rearrange("p j t -> p (j t)"))
            return codes, scales

        def score_pass(acc, picked, picked_scales, h_q, b, c):
            cols = slice(P * c, P * (c + 1))
            nc.tensor.matmul_mx(out=acc[:], lhsT=picked[:, cols].bitcast(FP8X4),
                                lhsT_scale=picked_scales[4 * (b + 1) :, cols],
                                rhs=h_q[0][:].bitcast(FP8X4), rhs_scale=h_q[1][:],
                                start=(b == 0), stop=(b == HP - 1))

        def pick3(b):
            return gather(tab_w["3", b][:].bitcast(U32), lists[2], U32, f"v3_w{b}", CFG["t3"].split()[b])

        def pick2(b):
            return gather(tab_w["2", b][:].bitcast(U32), lists[1], U32, f"v2_w{b}", CFG["t2"].split()[b])

        tie = dict(pair.split(":") for pair in CFG["tie"].split())
        if CFG["early"] == 0:
            w4_w.append(deal_words(1, "w4_w1"))
        v3_s = gather(tab3_sw[:], lists[2], U8, "v3_s")
        rows0 = features(0, 0)
        if CFG["early"] == 0:
            w4_w.append(deal_words(2, "w4_w0"))
        w1_q[1, 0] = quantise_w1(1, 0, "w1_codes01")
        w1_q[1, 1] = quantise_w1(1, 1, "ring1")
        h_q = [quantise_h(0, weave(rows0, tie.get("w0", "woven0"), CFG["il0"]), None)]
        v2_s = gather(tab2_sw[:], lists[1], U8, "v2_s")
        w1_q[2, 0] = quantise_w1(2, 0, "ring2")
        w1_q[2, 1] = quantise_w1(2, 1, "w1_codes01")
        v3_w = [pick3(0)]
        rows1 = features(1, 3)
        v3_w.append(pick3(1))
        rows2 = features(2, 3)
        v2_w = [pick2(0)]
        h_q.append(quantise_h(1, weave(rows1, "woven1", CFG["il"][0]), tie.get("h1")))
        v2_w.append(pick2(1))
        v3_w.append(pick3(2))
        h_q.append(quantise_h(2, weave(rows2, tie.get("w2", "woven0"), CFG["il"][1]), tie.get("h2")))
        v2_w.append(pick2(2))
        e3 = [psum.tile([P, S], F32, name=f"e3_{c}", tag=f"bank{4 + c}") for c in range(MT)]
        e2 = [psum.tile([P, S], F32, name=f"e2_{c}", tag=f"bank{c}") for c in range(MT)]
        for b in range(HP):
            for c in range(MT):
                score_pass(e3[c], v3_w[b], v3_s, h_q[b], b, c)
            for c in range(MT):
                score_pass(e2[c], v2_w[b], v2_s, h_q[b], b, c)
        larger, score = [], []
        for c in range(MT):
            e3_sb = held([P, S], F32, "e3_sb", f"ring{(c + 3) % 4}")
            nc.scalar.copy(out=e3_sb[:], in_=e3[c][:])
            larger.append(held([P, S], F32, "larger", f"final{c}"))
            nc.vector.tensor_tensor(out=larger[c][:], in0=e2[c][:], in1=e3_sb[:], op=ALU.max)
            score.append(held([P, S], F32, f"score{c}"))
            if c < CFG["gadd"]:
                scaled = held([P, S], F32, f"scaled{c}", f"h_rows{c}")
                nc.gpsimd.tensor_scalar(out=scaled[:], in0=e3_sb[:], scalar1=nav_sb[:, c : c + 1], scalar2=0.0,
                                        op0=ALU.mult, op1=ALU.add)
                nc.gpsimd.tensor_tensor(out=score[c][:], in0=scaled[:], in1=larger[c][:], op=ALU.add)
        for c in range(MT):
            if c >= CFG["gadd"]:
                nc.vector.scalar_tensor_tensor(out=score[c][:], in0=e3[c][:], scalar=nav_sb[:, c : c + 1], in1=larger[c][:],
                                               op0=ALU.mult, op1=ALU.add)
            nc.sync.dma_start(out=out[P * c : P * (c + 1), :], in_=score[c][:])
